import numpy as np
import ml_dtypes


def mxq(x, axis, fmt="e4m3"):
    dtype, down = {"e4m3": (ml_dtypes.float8_e4m3fn, 7), "e5m2": (ml_dtypes.float8_e5m2, 14)}[fmt]
    v = np.moveaxis(np.asarray(x, np.float32).astype(ml_dtypes.bfloat16).astype(np.float64), axis, -1)
    blocks = v.reshape(v.shape[:-1] + (-1, 32))
    amax = np.abs(blocks).max(-1, keepdims=True)
    byte = np.maximum(np.where(amax > 0, np.frexp(amax)[1] - 1 + 127, 0) - down, 1)
    scale = np.exp2(byte - 127.0)
    codes = (blocks / scale).astype(np.float32).astype(dtype).astype(np.float64)
    return np.moveaxis((codes * scale).reshape(v.shape), -1, axis)


WIDE = False


def mx_kscale(k):
    if not WIDE:
        return np.ones(k)
    levels = np.array([10, -10, 5, -5, 0])
    if k % 512:
        return np.exp2(np.random.permutation(np.resize(levels, k // 32))).repeat(32)
    a = np.empty((k // 512, 16))
    for p in range(k // 512):
        a[p, :8] = np.random.permutation(np.resize(levels, 8))
        for g in range(8):
            far = levels[np.abs(levels - a[p, g]) >= 10]
            a[p, g + 8] = far[np.random.randint(len(far))]
    return np.exp2(a.ravel()).repeat(32)


def f64(x):
    return np.asarray(x).astype(np.float64)


def striped(idx):
    return np.tile(np.asarray(idx).reshape(-1, 16).T, (8, 1)).astype(np.uint16)


def unstriped(offs):
    return offs[:16].T.reshape(-1).astype(np.int64)


E2M1 = np.array([0.0, 0.5, 1.0, 1.5, 2.0, 3.0, 4.0, 6.0, -0.0, -0.5, -1.0, -1.5, -2.0, -3.0, -4.0, -6.0])


def pack_weight(w, fmt):
    k, n = w.shape
    w = f64(np.asarray(w, np.float32).astype(ml_dtypes.bfloat16)).reshape(k // 32, 32, n)
    amax = np.abs(w).max(1)
    if fmt == "e4m3":
        byte = np.frexp(amax)[1] - 1 + 127 - 7
    else:
        mant, ex = np.frexp(amax / 6.0)
        byte = np.where(mant > 0.5, ex, ex - 1) + 127
    byte = np.clip(np.where(amax > 0, byte, 1), 1, 254)
    scaled = (w * np.exp2(127.0 - byte)[:, None, :]).reshape(k, n).astype(np.float32)
    by_word = np.ascontiguousarray(scaled.reshape(k // 512, 128, 4, n).transpose(0, 1, 3, 2))
    if fmt == "e4m3":
        words = by_word.astype(ml_dtypes.float8_e4m3fn).view(np.uint8)
    else:
        c = by_word.astype(ml_dtypes.float4_e2m1fn).view(np.uint8) & 0xF
        words = (c[..., 0::2] | (c[..., 1::2] << 4)).reshape(k // 512, 128, 2 * n)
    return np.ascontiguousarray(words), np.ascontiguousarray(byte.astype(np.uint8).reshape(k // 512, 16, n))


def unpack_weight(words, scales, fmt):
    g, _, n = scales.shape
    words = np.ascontiguousarray(words).reshape(g, 128, n, -1)
    if fmt == "e4m3":
        vals = words.view(ml_dtypes.float8_e4m3fn).astype(np.float64)
    else:
        nib = np.empty((g, 128, n, 4), np.uint8)
        nib[..., 0::2] = words & 0xF
        nib[..., 1::2] = words >> 4
        vals = E2M1[nib]
    vals = vals * np.repeat(np.exp2(scales.astype(np.float64) - 127.0), 8, axis=1)[..., None]
    return vals.transpose(0, 1, 3, 2).reshape(g * 512, n)


D, T, I, Q, E, M = 512, 2048, 512, 256, 512, 1024


def setup_inputs():
    n = np.random.standard_normal
    idx = np.random.permutation(T)[:I]
    idx2 = np.random.permutation(T)[:I]
    idx3 = np.random.permutation(T)[:I]
    idx4 = np.random.permutation(M)[:Q]
    fd = mx_kscale(D)
    fi = mx_kscale(I)
    ti = np.ones(T)
    ti[idx] = fi
    keysp = pack_weight(n((D, T)) / fd[:, None], "e4m3")
    return {
        "query": (n((D, Q)) * 1.2 / np.sqrt(D) * fd[:, None]).astype(np.float32),
        "keys_words": keysp[0],
        "keys_scales": keysp[1],
        "lam": (np.random.uniform(0.8, 1.8, (Q, 1))).astype(np.float32),
        "os": (np.random.uniform(0.02, 0.08, (1, I)) * fi).astype(np.float32),
        "vals": (n((E, T)) / ti).astype(np.float32),
        "member": (n((E, M))).astype(np.float32),
        "mgain": np.tile(np.random.uniform(0.5, 2.0, M), (128, 1)).astype(np.float32),
        "offs": striped(idx),
        "offs2": striped(idx2),
        "offs3": striped(idx3),
        "offs4": striped(idx4),
    }


def reference(query, keys_words, keys_scales, lam, os, vals, member, mgain, offs, offs2, offs3, offs4):
    idx = unstriped(offs)
    idx2 = unstriped(offs2)
    idx3 = unstriped(offs3)
    idx4 = unstriped(offs4)
    keysu = unpack_weight(keys_words, keys_scales, "e4m3")
    queryq = mxq(f64(query), 0, "e4m3")
    a = queryq.T @ keysu
    lo2 = np.minimum(a[:, idx], a[:, idx2])
    hi2 = np.maximum(a[:, idx], a[:, idx2])
    s = np.maximum(lo2, np.minimum(hi2, a[:, idx3])) * f64(lam)
    w = np.maximum(s, 0.0)
    wo1 = w * f64(os)
    wt1 = wo1.T
    vt1 = f64(vals)[:, idx].T
    vt1q = mxq(vt1, 0, "e4m3")
    wt1q = mxq(wt1, 0, "e4m3")
    o = vt1q.T @ wt1q
    y = o * f64(mgain)[:1][:, idx4] + f64(member)[:, idx4]
    return y

@@ -1,0 +1,265 @@
+from contextlib import ExitStack
+
+import concourse.mybir as mybir
+from concourse.masks import make_identity
+
+D, T, I, Q, E, M = 512, 2048, 512, 256, 512, 1024
+FLOPS = 2 * D * Q * T + 2 * I * E * Q
+
+F32 = mybir.dt.float32
+BF16 = mybir.dt.bfloat16
+U32 = mybir.dt.uint32
+I32 = mybir.dt.int32
+U16 = mybir.dt.uint16
+U8 = mybir.dt.uint8
+FP8X4 = mybir.dt.float8_e4m3fn_x4
+ALU = mybir.AluOpType
+COPY = mybir.ActivationFunctionType.Copy
+
+P = 128
+PACK = 4
+BANK = 512
+QT = Q // P
+EB = E // P
+CH = T // BANK
+
+
+def tile_attend_middle_bymember_lean_kernel(
+    tc, query, keys_words, keys_scales, lam, slot_factor, vals, member, mgain, offs, offs2, offs3, offs4, out
+):
+    nc = tc.nc
+    with ExitStack() as ctx:
+        keep = ctx.enter_context(tc.tile_pool(name="keep", bufs=1))
+        psum = ctx.enter_context(tc.psum_pool(name="psum", bufs=1))
+
+        def sb(name, shape, dtype, tag=""):
+            return keep.tile(shape, dtype, name=name, tag=tag or name, align_bytes=64)
+
+        def bank(tag, shape, name):
+            return psum.tile(shape, F32, name=name, tag=tag)
+
+        k_scales = sb("k_scales", [P, BANK], U8)
+        nc.gpsimd.memset(k_scales[:].bitcast(I32), 0)
+        ident = sb("ident", [P, P], F32)
+        make_identity(nc, ident[:])
+
+        q_raw = [sb(f"q_raw{j}", [P, PACK, P], F32) for j in range(QT)]
+        half = T // 2
+        k_words = [sb(f"k_words{h}", [P, half], U32) for h in range(2)]
+        k_flat = keys_words[0].rearrange("p n t -> p (n t)")
+
+        def load_query(j):
+            nc.sync.dma_start(q_raw[j][:], query[:, P * j : P * (j + 1)].rearrange("(p t) q -> p t q", t=PACK))
+
+        load_query(0)
+        for quad in range(4):
+            rows = keys_scales[0][4 * quad : 4 * quad + 4, :].bitcast(I32)
+            queue = nc.sync if quad < 2 else nc.scalar
+            queue.dma_start(
+                k_scales[32 * quad : 32 * quad + 16, :].bitcast(I32),
+                rows.rearrange("r (c n) -> c r n", c=CH),
+            )
+        for h in range(2):
+            nc.sync.dma_start(
+                k_words[h][:].bitcast(I32), k_flat[:, PACK * half * h : PACK * half * (h + 1)].bitcast(I32)
+            )
+        load_query(1)
+        lists = []
+        for n, src in enumerate((offs, offs2, offs3)):
+            lists.append(keep.tile([P, I // 16], U16, name=f"list{n}"))
+            nc.sync.dma_start(lists[n][:], src)
+        v_pool = [sb(f"v_pool{b}", [P, T], F32) for b in range(EB)]
+        m_pool = [sb(f"m_pool{b}", [P, M], F32) for b in range(EB)]
+        for b in range(2):
+            nc.sync.dma_start(v_pool[b][:], vals[P * b : P * (b + 1), :])
+        lam_col = sb("lam_col", [P, QT], F32)
+        with nc.allow_non_contiguous_dma(reason="one factor a partition"):
+            nc.sync.dma_start(lam_col[:], lam.rearrange("(j p) o -> p (j o)", j=QT))
+        os_col = sb("os_col", [P, PACK], F32)
+        nc.sync.dma_start(os_col[:], slot_factor.rearrange("o (p t) -> (o p) t", t=PACK))
+        list4 = keep.tile([P, Q // 16], U16, name="list4")
+        nc.sync.dma_start(list4[:], offs4)
+        g_pool = sb("g_pool", [P, M], F32)
+        nc.sync.dma_start(g_pool[:], mgain)
+        for b in range(2, EB):
+            nc.sync.dma_start(v_pool[b][:], vals[P * b : P * (b + 1), :])
+        for b in range(EB):
+            nc.sync.dma_start(m_pool[b][:], member[P * b : P * (b + 1), :])
+
+        q_bf = [sb(f"q_bf{j}", [P, P, PACK], BF16) for j in range(QT)]
+        q_codes = [sb(f"q_codes{j}", [P, P], U32) for j in range(QT)]
+        q_scales = [sb(f"q_scales{j}", [P, P], U8) for j in range(QT)]
+
+        def q_view(j):
+            return q_raw[j][:].rearrange("p t q -> p q t")
+
+        def quantize(codes, scales, src):
+            nc.vector.quantize_mx(out=codes.bitcast(FP8X4), scales=scales, in_=src)
+
+        def prepare_query(j):
+            nc.vector.tensor_copy(q_bf[j][:], q_view(j))
+            quantize(q_codes[j][:], q_scales[j][:], q_bf[j][:].rearrange("p q t -> p (q t)"))
+
+        a_sb = [sb(f"a_sb{j}", [P, T], F32) for j in range(QT)]
+        picked = [[sb(f"picked{j}_{n}", [P, I], F32) for n in range(3)] for j in range(QT)]
+
+        def scores(j, c, on_vector):
+            acc = bank(f"acc{c}", [P, BANK], f"a_ps{j}_{c}")
+            nc.tensor.matmul_mx(
+                out=acc[:],
+                lhsT=q_codes[j][:].bitcast(FP8X4),
+                lhsT_scale=q_scales[j][:],
+                rhs=k_words[c // 2][:, BANK * (c % 2) : BANK * (c % 2 + 1)].bitcast(FP8X4),
+                rhs_scale=k_scales[4 * c :, :],
+                start=True,
+                stop=True,
+            )
+            dst = a_sb[j][:, BANK * c : BANK * (c + 1)]
+            if on_vector:
+                nc.vector.tensor_copy(dst, acc[:])
+            else:
+                nc.scalar.activation(dst, acc[:], COPY)
+
+        def pick(j, n, on_vector):
+            src = a_sb[j][:].indirect(lists[n][:])
+            if on_vector:
+                nc.vector.tensor_copy(picked[j][n][:], src)
+            else:
+                nc.scalar.activation(picked[j][n][:], src, COPY)
+
+        w_bf = sb("w_bf", [P, Q, PACK], BF16)
+        w_codes = sb("w_codes", [P, Q], U32)
+        w_scales = sb("w_scales", [P, Q], U8)
+        relu_s = [sb(f"relu_s{j}", [P, I], F32) for j in range(QT)]
+
+        pair = {}
+
+        def order_pair(j):
+            g1, g2, g3 = picked[j]
+            pair[j] = sb(f"pair{j}", [P, 2, I], F32, "pair")
+            nc.vector.tensor_tensor(pair[j][:, 1, :], g1[:], g2[:], ALU.max)
+            nc.vector.tensor_tensor(pair[j][:, 0, :], g1[:], g2[:], ALU.min)
+
+        def cap(j):
+            nc.vector.tensor_tensor(pair[j][:, 1, :], pair[j][:, 1, :], picked[j][2][:], ALU.min)
+
+        def median(j):
+            nc.vector.tensor_tensor(pair[j][:, 0, :], pair[j][:, 0, :], pair[j][:, 1, :], ALU.max)
+
+        def positive(j):
+            nc.vector.tensor_scalar(
+                relu_s[j][:].rearrange("p (t s) -> p s t", t=PACK),
+                pair[j][:, 0, :].rearrange("p (s t) -> p s t", t=PACK),
+                lam_col[:, j : j + 1],
+                0.0,
+                ALU.mult,
+                ALU.max,
+            )
+            for t in range(PACK):
+                nc.tensor.transpose(w_ps[j][:, t, :], relu_s[j][:, P * t : P * (t + 1)], ident[:])
+
+        w_ps = [bank(f"w_ps{j}", [P, PACK, P], f"w_ps{j}") for j in range(QT)]
+
+        def weave_weights(j):
+            nc.vector.tensor_tensor(
+                w_bf[:, P * j : P * (j + 1), :],
+                w_ps[j][:].rearrange("p t q -> p q t"),
+                os_col[:].unsqueeze(1).to_broadcast([P, P, PACK]),
+                ALU.mult,
+            )
+
+        v_in = {}
+        v_codes = {}
+        v_scales = [sb(f"v_scales{g}", [P, 2 * P], U8) for g in range(2)]
+
+        v_ps = [bank(f"v_ps{g}", [P, 2, 2, P], f"v_ps{g}") for g in range(2)]
+
+        def pick_values(b, on_vector, tag=""):
+            v_bf = sb(f"v_bf{b}", [P, I], BF16, tag)
+            src = v_pool[b][:].indirect(lists[0][:])
+            if on_vector:
+                nc.vector.tensor_copy(v_bf[:], src)
+            else:
+                nc.scalar.activation(v_bf[:], src, COPY)
+            words = v_bf[:].bitcast(F32)
+            for u in range(2):
+                nc.tensor.transpose(v_ps[b // 2][:, b % 2, u, :], words[:, u::2], ident[:])
+
+        def weave_values(g, tag):
+            v_in[g] = sb(f"v_in{g}", [P, 2, P, 2], F32, tag)
+            nc.scalar.copy(v_in[g][:], v_ps[g][:].rearrange("p x u e -> p x e u"))
+
+        def quantize_values(g, tag):
+            v_codes[g] = sb(f"v_codes{g}", [P, 2 * P], U32, tag)
+            quantize(v_codes[g][:], v_scales[g][:], v_in[g][:].rearrange("p x e u -> p (x e u)").bitcast(BF16))
+
+        m_picked = [sb(f"m_picked{b}", [P, Q], F32) for b in range(EB)]
+        scaled = [sb(f"scaled{g}", [P, 2, Q], F32) for g in range(2)]
+        result = [sb(f"result{b}", [P, Q], F32) for b in range(EB)]
+
+        def pick_member(b):
+            nc.scalar.activation(m_picked[b][:], m_pool[b][:].indirect(list4[:]), COPY)
+
+        def product(g):
+            acc = bank(f"v_ps{1 - g}", [P, 2, Q], f"o_ps{g}")
+            for x in range(2):
+                nc.tensor.matmul_mx(
+                    out=acc[:, x, :],
+                    lhsT=v_codes[g][:, P * x : P * (x + 1)].bitcast(FP8X4),
+                    lhsT_scale=v_scales[g][:, P * x : P * (x + 1)],
+                    rhs=w_codes[:].bitcast(FP8X4),
+                    rhs_scale=w_scales[:],
+                    start=True,
+                    stop=True,
+                )
+            nc.vector.tensor_tensor(
+                scaled[g][:], acc[:], gain[:].unsqueeze(1).to_broadcast([P, 2, Q]), ALU.mult
+            )
+
+        def finish(b):
+            nc.vector.tensor_tensor(result[b][:], scaled[b // 2][:, b % 2, :], m_picked[b][:], ALU.add)
+            nc.sync.dma_start(out[P * b : P * (b + 1), :], result[b][:])
+
+        prepare_query(0)
+        for c in range(CH - 1):
+            scores(0, c, c == 0)
+        prepare_query(1)
+        scores(0, CH - 1, True)
+        pick(0, 0, True)
+        pick(0, 1, False)
+        pick(0, 2, False)
+        for c in range(CH):
+            scores(1, c, c < 2)
+        order_pair(0)
+        cap(0)
+        pick_values(0, True)
+        median(0)
+        positive(0)
+        for n in range(3):
+            pick(1, n, False)
+        order_pair(1)
+        weave_weights(0)
+        cap(1)
+        gain = sb("gain", [P, Q], F32, "picked1_2")
+        nc.vector.tensor_copy(gain[:], g_pool[:].indirect(list4[:]))
+        median(1)
+        positive(1)
+        pick_values(1, False, "relu_s0")
+        pick_values(2, False)
+        weave_values(0, "v_pool2")
+        quantize_values(0, "pair")
+        weave_weights(1)
+        quantize(w_codes[:], w_scales[:], w_bf[:].rearrange("p q t -> p (q t)"))
+        pick_values(3, False)
+        pick_member(0)
+        weave_values(1, "m_pool0")
+        product(0)
+        finish(0)
+        quantize_values(1, "w_bf")
+        pick_member(1)
+        finish(1)
+        product(1)
+        pick_member(2)
+        pick_member(3)
+        finish(2)
+        finish(3)

@@ -70,8 +70,11 @@ def tile_attend_middle_bymember_lean_kernel(
             nc.sync.dma_start(lists[n][:], src)
         v_pool = [sb(f"v_pool{b}", [P, T], F32) for b in range(EB)]
         m_pool = [sb(f"m_pool{b}", [P, M], F32) for b in range(EB)]
-        for b in range(2):
+
+        def load_values(b):
             nc.sync.dma_start(v_pool[b][:], vals[P * b : P * (b + 1), :])
+
+        load_values(0)
         lam_col = sb("lam_col", [P, QT], F32)
         with nc.allow_non_contiguous_dma(reason="one factor a partition"):
             nc.sync.dma_start(lam_col[:], lam.rearrange("(j p) o -> p (j o)", j=QT))
@@ -79,10 +82,10 @@ def tile_attend_middle_bymember_lean_kernel(
         nc.sync.dma_start(os_col[:], slot_factor.rearrange("o (p t) -> (o p) t", t=PACK))
         list4 = keep.tile([P, Q // 16], U16, name="list4")
         nc.sync.dma_start(list4[:], offs4)
+        for b in range(1, EB):
+            load_values(b)
         g_pool = sb("g_pool", [P, M], F32)
         nc.sync.dma_start(g_pool[:], mgain)
-        for b in range(2, EB):
-            nc.sync.dma_start(v_pool[b][:], vals[P * b : P * (b + 1), :])
         for b in range(EB):
             nc.sync.dma_start(m_pool[b][:], member[P * b : P * (b + 1), :])
 
@@ -90,14 +93,14 @@ def tile_attend_middle_bymember_lean_kernel(
         q_codes = [sb(f"q_codes{j}", [P, P], U32) for j in range(QT)]
         q_scales = [sb(f"q_scales{j}", [P, P], U8) for j in range(QT)]
 
-        def q_view(j):
-            return q_raw[j][:].rearrange("p t q -> p q t")
-
         def quantize(codes, scales, src):
             nc.vector.quantize_mx(out=codes.bitcast(FP8X4), scales=scales, in_=src)
 
         def prepare_query(j):
-            nc.vector.tensor_copy(q_bf[j][:], q_view(j))
+            nc.vector.tensor_copy(
+                q_bf[j][:].rearrange("p (c n) t -> p c t n", n=4),
+                q_raw[j][:].rearrange("p t (c n) -> p c t n", n=4),
+            )
             quantize(q_codes[j][:], q_scales[j][:], q_bf[j][:].rearrange("p q t -> p (q t)"))
 
         a_sb = [sb(f"a_sb{j}", [P, T], F32) for j in range(QT)]
@@ -127,29 +130,33 @@ def tile_attend_middle_bymember_lean_kernel(
             else:
                 nc.scalar.activation(picked[j][n][:], src, COPY)
 
-        w_bf = sb("w_bf", [P, Q, PACK], BF16)
+        w_bf = {}
         w_codes = sb("w_codes", [P, Q], U32)
         w_scales = sb("w_scales", [P, Q], U8)
         relu_s = [sb(f"relu_s{j}", [P, I], F32) for j in range(QT)]
 
-        pair = {}
+        lo = [sb(f"lo{j}", [P, I], F32) for j in range(QT)]
+        hi = [sb(f"hi{j}", [P, I], F32) for j in range(QT)]
 
-        def order_pair(j):
-            g1, g2, g3 = picked[j]
-            pair[j] = sb(f"pair{j}", [P, 2, I], F32, "pair")
-            nc.vector.tensor_tensor(pair[j][:, 1, :], g1[:], g2[:], ALU.max)
-            nc.vector.tensor_tensor(pair[j][:, 0, :], g1[:], g2[:], ALU.min)
+        def larger(j):
+            nc.vector.tensor_tensor(hi[j][:], picked[j][0][:], picked[j][1][:], ALU.max)
+
+        def smaller(j):
+            nc.vector.tensor_tensor(lo[j][:], picked[j][0][:], picked[j][1][:], ALU.min)
 
         def cap(j):
-            nc.vector.tensor_tensor(pair[j][:, 1, :], pair[j][:, 1, :], picked[j][2][:], ALU.min)
+            nc.vector.tensor_tensor(hi[j][:], hi[j][:], picked[j][2][:], ALU.min)
 
-        def median(j):
-            nc.vector.tensor_tensor(pair[j][:, 0, :], pair[j][:, 0, :], pair[j][:, 1, :], ALU.max)
+        middle = {}
+
+        def median(j, tag):
+            middle[j] = sb(f"middle{j}", [P, I], F32, tag)
+            nc.vector.tensor_tensor(middle[j][:], lo[j][:], hi[j][:], ALU.max)
 
         def positive(j):
             nc.vector.tensor_scalar(
-                relu_s[j][:].rearrange("p (t s) -> p s t", t=PACK),
-                pair[j][:, 0, :].rearrange("p (s t) -> p s t", t=PACK),
+                relu_s[j][:].rearrange("p (t c n) -> p c t n", t=PACK, n=4),
+                middle[j][:].rearrange("p (c n t) -> p c t n", t=PACK, n=4),
                 lam_col[:, j : j + 1],
                 0.0,
                 ALU.mult,
@@ -160,48 +167,54 @@ def tile_attend_middle_bymember_lean_kernel(
 
         w_ps = [bank(f"w_ps{j}", [P, PACK, P], f"w_ps{j}") for j in range(QT)]
 
-        def weave_weights(j):
+        def quantize_weights(j):
+            cols = slice(P * j, P * (j + 1))
+            quantize(w_codes[:, cols], w_scales[:, cols], w_bf[j][:].rearrange("p q t -> p (q t)"))
+
+        def weave_weights(j, tag):
+            w_bf[j] = sb(f"w_bf{j}", [P, P, PACK], BF16, tag)
             nc.vector.tensor_tensor(
-                w_bf[:, P * j : P * (j + 1), :],
+                w_bf[j][:],
                 w_ps[j][:].rearrange("p t q -> p q t"),
                 os_col[:].unsqueeze(1).to_broadcast([P, P, PACK]),
                 ALU.mult,
             )
 
         v_in = {}
-        v_codes = {}
+        v_codes = [sb(f"v_codes{g}", [P, 2 * P], U32) for g in range(2)]
         v_scales = [sb(f"v_scales{g}", [P, 2 * P], U8) for g in range(2)]
 
-        v_ps = [bank(f"v_ps{g}", [P, 2, 2, P], f"v_ps{g}") for g in range(2)]
+        v_ps = {}
+        v_bf = [sb(f"v_bf{b}", [P, I], BF16) for b in range(EB)]
 
-        def pick_values(b, on_vector, tag=""):
-            v_bf = sb(f"v_bf{b}", [P, I], BF16, tag)
+        def pick_values(b, on_vector):
             src = v_pool[b][:].indirect(lists[0][:])
             if on_vector:
-                nc.vector.tensor_copy(v_bf[:], src)
+                nc.vector.tensor_copy(v_bf[b][:], src)
             else:
-                nc.scalar.activation(v_bf[:], src, COPY)
-            words = v_bf[:].bitcast(F32)
+                nc.scalar.activation(v_bf[b][:], src, COPY)
+
+        def turn_values(b):
+            words = v_bf[b][:].bitcast(F32)
             for u in range(2):
                 nc.tensor.transpose(v_ps[b // 2][:, b % 2, u, :], words[:, u::2], ident[:])
 
-        def weave_values(g, tag):
+        def weave_values(g, tag, copy):
             v_in[g] = sb(f"v_in{g}", [P, 2, P, 2], F32, tag)
-            nc.scalar.copy(v_in[g][:], v_ps[g][:].rearrange("p x u e -> p x e u"))
+            copy(v_in[g][:], v_ps[g][:].rearrange("p x u e -> p x e u"))
 
-        def quantize_values(g, tag):
-            v_codes[g] = sb(f"v_codes{g}", [P, 2 * P], U32, tag)
+        def quantize_values(g):
             quantize(v_codes[g][:], v_scales[g][:], v_in[g][:].rearrange("p x e u -> p (x e u)").bitcast(BF16))
 
-        m_picked = [sb(f"m_picked{b}", [P, Q], F32) for b in range(EB)]
+        m_picked = [sb(f"m_picked{g}", [P, 2, Q], F32) for g in range(2)]
         scaled = [sb(f"scaled{g}", [P, 2, Q], F32) for g in range(2)]
-        result = [sb(f"result{b}", [P, Q], F32) for b in range(EB)]
+        result = [sb(f"result{g}", [P, 2, Q], F32) for g in range(2)]
 
         def pick_member(b):
-            nc.scalar.activation(m_picked[b][:], m_pool[b][:].indirect(list4[:]), COPY)
+            nc.scalar.activation(m_picked[b // 2][:, b % 2, :], m_pool[b][:].indirect(list4[:]), COPY)
 
-        def product(g):
-            acc = bank(f"v_ps{1 - g}", [P, 2, Q], f"o_ps{g}")
+        def product(g, tag):
+            acc = bank(tag, [P, 2, Q], f"o_ps{g}")
             for x in range(2):
                 nc.tensor.matmul_mx(
                     out=acc[:, x, :],
@@ -217,8 +230,9 @@ def tile_attend_middle_bymember_lean_kernel(
             )
 
         def finish(b):
-            nc.vector.tensor_tensor(result[b][:], scaled[b // 2][:, b % 2, :], m_picked[b][:], ALU.add)
-            nc.sync.dma_start(out[P * b : P * (b + 1), :], result[b][:])
+            g, x = divmod(b, 2)
+            nc.vector.tensor_tensor(result[g][:, x, :], scaled[g][:, x, :], m_picked[g][:, x, :], ALU.add)
+            nc.sync.dma_start(out[P * b : P * (b + 1), :], result[g][:, x, :])
 
         prepare_query(0)
         for c in range(CH - 1):
@@ -230,36 +244,38 @@ def tile_attend_middle_bymember_lean_kernel(
         pick(0, 2, False)
         for c in range(CH):
             scores(1, c, c < 2)
-        order_pair(0)
+        larger(0)
+        smaller(0)
         cap(0)
         pick_values(0, True)
-        median(0)
+        median(0, "v_pool0")
         positive(0)
         for n in range(3):
             pick(1, n, False)
-        order_pair(1)
-        weave_weights(0)
+        larger(1)
+        smaller(1)
         cap(1)
-        gain = sb("gain", [P, Q], F32, "picked1_2")
-        nc.vector.tensor_copy(gain[:], g_pool[:].indirect(list4[:]))
-        median(1)
+        weave_weights(0, "picked1_0")
+        median(1, "")
         positive(1)
-        pick_values(1, False, "relu_s0")
-        pick_values(2, False)
-        weave_values(0, "v_pool2")
-        quantize_values(0, "pair")
-        weave_weights(1)
-        quantize(w_codes[:], w_scales[:], w_bf[:].rearrange("p q t -> p (q t)"))
-        pick_values(3, False)
-        pick_member(0)
-        weave_values(1, "m_pool0")
-        product(0)
-        finish(0)
-        quantize_values(1, "w_bf")
-        pick_member(1)
-        finish(1)
-        product(1)
-        pick_member(2)
-        pick_member(3)
-        finish(2)
-        finish(3)
+        quantize_weights(0)
+        v_ps[0] = bank("w_ps0", [P, 2, 2, P], "v_ps0")
+        v_ps[1] = bank("v_ps1", [P, 2, 2, P], "v_ps1")
+        turn_values(0)
+        for b in range(1, EB):
+            pick_values(b, False)
+            turn_values(b)
+        weave_values(0, "hi1", nc.vector.tensor_copy)
+        weave_weights(1, "")
+        quantize_weights(1)
+        quantize_values(0)
+        gain = sb("gain", [P, Q], F32)
+        nc.scalar.activation(gain[:], g_pool[:].indirect(list4[:]), COPY)
+        weave_values(1, "g_pool", nc.scalar.copy)
+        quantize_values(1)
+        product(0, "v_ps1")
+        product(1, "acc0")
+        for b in range(EB):
+            pick_member(b)
+        for b in range(EB):
+            finish(b)

@@ -44,8 +44,7 @@ def tile_attend_middle_bymember_lean_kernel(
         make_identity(nc, ident[:])
 
         q_raw = [sb(f"q_raw{j}", [P, PACK, P], F32) for j in range(QT)]
-        half = T // 2
-        k_words = [sb(f"k_words{h}", [P, half], U32) for h in range(2)]
+        k_words = [sb(f"k_words{c}", [P, BANK], U32) for c in range(CH)]
         k_flat = keys_words[0].rearrange("p n t -> p (n t)")
 
         def load_query(j):
@@ -59,9 +58,9 @@ def tile_attend_middle_bymember_lean_kernel(
                 k_scales[32 * quad : 32 * quad + 16, :].bitcast(I32),
                 rows.rearrange("r (c n) -> c r n", c=CH),
             )
-        for h in range(2):
+        for c in range(CH):
             nc.sync.dma_start(
-                k_words[h][:].bitcast(I32), k_flat[:, PACK * half * h : PACK * half * (h + 1)].bitcast(I32)
+                k_words[c][:].bitcast(I32), k_flat[:, PACK * BANK * c : PACK * BANK * (c + 1)].bitcast(I32)
             )
         load_query(1)
         lists = []
@@ -74,10 +73,10 @@ def tile_attend_middle_bymember_lean_kernel(
         def load_values(b):
             nc.sync.dma_start(v_pool[b][:], vals[P * b : P * (b + 1), :])
 
-        load_values(0)
         lam_col = sb("lam_col", [P, QT], F32)
         with nc.allow_non_contiguous_dma(reason="one factor a partition"):
             nc.sync.dma_start(lam_col[:], lam.rearrange("(j p) o -> p (j o)", j=QT))
+        load_values(0)
         os_col = sb("os_col", [P, PACK], F32)
         nc.sync.dma_start(os_col[:], slot_factor.rearrange("o (p t) -> (o p) t", t=PACK))
         list4 = keep.tile([P, Q // 16], U16, name="list4")
@@ -104,26 +103,28 @@ def tile_attend_middle_bymember_lean_kernel(
             quantize(q_codes[j][:], q_scales[j][:], q_bf[j][:].rearrange("p q t -> p (q t)"))
 
         a_sb = [sb(f"a_sb{j}", [P, T], F32) for j in range(QT)]
-        picked = [[sb(f"picked{j}_{n}", [P, I], F32) for n in range(3)] for j in range(QT)]
+        picked = [{} for j in range(QT)]
 
-        def scores(j, c, on_vector):
-            acc = bank(f"acc{c}", [P, BANK], f"a_ps{j}_{c}")
+        def scores(j, c, on_vector, first=0, width=BANK, tag=""):
+            acc = bank(tag or f"acc{c}", [P, width], f"a_ps{j}_{c}_{first}")
+            cols = slice(first, first + width)
             nc.tensor.matmul_mx(
                 out=acc[:],
                 lhsT=q_codes[j][:].bitcast(FP8X4),
                 lhsT_scale=q_scales[j][:],
-                rhs=k_words[c // 2][:, BANK * (c % 2) : BANK * (c % 2 + 1)].bitcast(FP8X4),
-                rhs_scale=k_scales[4 * c :, :],
+                rhs=k_words[c][:, cols].bitcast(FP8X4),
+                rhs_scale=k_scales[4 * c :, cols],
                 start=True,
                 stop=True,
             )
-            dst = a_sb[j][:, BANK * c : BANK * (c + 1)]
+            dst = a_sb[j][:, BANK * c + first : BANK * c + first + width]
             if on_vector:
                 nc.vector.tensor_copy(dst, acc[:])
             else:
                 nc.scalar.activation(dst, acc[:], COPY)
 
-        def pick(j, n, on_vector):
+        def pick(j, n, on_vector, tag=""):
+            picked[j][n] = sb(f"picked{j}_{n}", [P, I], F32, tag)
             src = a_sb[j][:].indirect(lists[n][:])
             if on_vector:
                 nc.vector.tensor_copy(picked[j][n][:], src)
@@ -133,37 +134,40 @@ def tile_attend_middle_bymember_lean_kernel(
         w_bf = {}
         w_codes = sb("w_codes", [P, Q], U32)
         w_scales = sb("w_scales", [P, Q], U8)
-        relu_s = [sb(f"relu_s{j}", [P, I], F32) for j in range(QT)]
+        lo = {}
+        hi = {}
 
-        lo = [sb(f"lo{j}", [P, I], F32) for j in range(QT)]
-        hi = [sb(f"hi{j}", [P, I], F32) for j in range(QT)]
+        second = [sb(f"second{j}", [P, I], F32) for j in range(QT)]
 
-        def larger(j):
-            nc.vector.tensor_tensor(hi[j][:], picked[j][0][:], picked[j][1][:], ALU.max)
+        def scale_second(j):
+            nc.gpsimd.tensor_scalar(second[j][:], picked[j][1][:], lam_col[:, j : j + 1], 0.0, ALU.mult, ALU.add)
 
-        def smaller(j):
-            nc.vector.tensor_tensor(lo[j][:], picked[j][0][:], picked[j][1][:], ALU.min)
+        def scaled_against(dst, j, n, other, op):
+            nc.vector.scalar_tensor_tensor(dst, picked[j][n][:], lam_col[:, j : j + 1], other, ALU.mult, op)
+
+        def larger(j, tag):
+            hi[j] = sb(f"hi{j}", [P, I], F32, tag)
+            scaled_against(hi[j][:], j, 0, second[j][:], ALU.max)
+
+        def smaller(j, tag):
+            lo[j] = sb(f"lo{j}", [P, I], F32, tag)
+            scaled_against(lo[j][:], j, 0, second[j][:], ALU.min)
 
         def cap(j):
-            nc.vector.tensor_tensor(hi[j][:], hi[j][:], picked[j][2][:], ALU.min)
+            scaled_against(hi[j][:], j, 2, hi[j][:], ALU.min)
 
         middle = {}
 
-        def median(j, tag):
-            middle[j] = sb(f"middle{j}", [P, I], F32, tag)
-            nc.vector.tensor_tensor(middle[j][:], lo[j][:], hi[j][:], ALU.max)
-
-        def positive(j):
-            nc.vector.tensor_scalar(
-                relu_s[j][:].rearrange("p (t c n) -> p c t n", t=PACK, n=4),
-                middle[j][:].rearrange("p (c n t) -> p c t n", t=PACK, n=4),
-                lam_col[:, j : j + 1],
-                0.0,
-                ALU.mult,
+        def median(j):
+            middle[j] = sb(f"middle{j}", [P, 2, I // 2], F32)
+            nc.vector.tensor_tensor(
+                middle[j][:],
+                lo[j][:].rearrange("p (m u) -> p u m", u=2),
+                hi[j][:].rearrange("p (m u) -> p u m", u=2),
                 ALU.max,
             )
             for t in range(PACK):
-                nc.tensor.transpose(w_ps[j][:, t, :], relu_s[j][:, P * t : P * (t + 1)], ident[:])
+                nc.tensor.transpose(w_ps[j][:, t, :], middle[j][:, t % 2, t // 2 :: 2], ident[:])
 
         w_ps = [bank(f"w_ps{j}", [P, PACK, P], f"w_ps{j}") for j in range(QT)]
 
@@ -173,10 +177,12 @@ def tile_attend_middle_bymember_lean_kernel(
 
         def weave_weights(j, tag):
             w_bf[j] = sb(f"w_bf{j}", [P, P, PACK], BF16, tag)
-            nc.vector.tensor_tensor(
+            nc.vector.scalar_tensor_tensor(
                 w_bf[j][:],
                 w_ps[j][:].rearrange("p t q -> p q t"),
+                0.0,
                 os_col[:].unsqueeze(1).to_broadcast([P, P, PACK]),
+                ALU.max,
                 ALU.mult,
             )
 
@@ -185,9 +191,10 @@ def tile_attend_middle_bymember_lean_kernel(
         v_scales = [sb(f"v_scales{g}", [P, 2 * P], U8) for g in range(2)]
 
         v_ps = {}
-        v_bf = [sb(f"v_bf{b}", [P, I], BF16) for b in range(EB)]
+        v_bf = {}
 
-        def pick_values(b, on_vector):
+        def pick_values(b, on_vector, tag):
+            v_bf[b] = sb(f"v_bf{b}", [P, I], BF16, tag)
             src = v_pool[b][:].indirect(lists[0][:])
             if on_vector:
                 nc.vector.tensor_copy(v_bf[b][:], src)
@@ -236,44 +243,49 @@ def tile_attend_middle_bymember_lean_kernel(
 
         prepare_query(0)
         for c in range(CH - 1):
-            scores(0, c, c == 0)
+            scores(0, c, c != 1)
+        scores(0, CH - 1, False, 0, BANK // 2)
+        scores(0, CH - 1, False, BANK // 2, BANK // 2, "acc4")
         prepare_query(1)
-        scores(0, CH - 1, True)
-        pick(0, 0, True)
+        pick(0, 0, True, "q_bf1")
         pick(0, 1, False)
+        scale_second(0)
         pick(0, 2, False)
         for c in range(CH):
             scores(1, c, c < 2)
-        larger(0)
-        smaller(0)
+        larger(0, "")
+        smaller(0, "")
         cap(0)
-        pick_values(0, True)
-        median(0, "v_pool0")
-        positive(0)
-        for n in range(3):
-            pick(1, n, False)
-        larger(1)
-        smaller(1)
-        cap(1)
-        weave_weights(0, "picked1_0")
-        median(1, "")
-        positive(1)
-        quantize_weights(0)
-        v_ps[0] = bank("w_ps0", [P, 2, 2, P], "v_ps0")
-        v_ps[1] = bank("v_ps1", [P, 2, 2, P], "v_ps1")
+        median(0)
+        v_ps[0] = bank("acc4", [P, 2, 2, P], "v_ps0")
+        pick_values(0, True, "picked0_2")
         turn_values(0)
-        for b in range(1, EB):
-            pick_values(b, False)
-            turn_values(b)
-        weave_values(0, "hi1", nc.vector.tensor_copy)
+        pick(1, 1, False)
+        scale_second(1)
+        pick(1, 0, False)
+        pick(1, 2, False)
+        larger(1, "lo0")
+        smaller(1, "hi0")
+        cap(1)
+        median(1)
+        pick_values(1, False, "v_pool0")
+        turn_values(1)
+        pick_values(2, False, "picked0_2")
+        pick_values(3, False, "v_pool1")
+        weave_weights(0, "picked1_2")
+        v_ps[1] = bank("w_ps0", [P, 2, 2, P], "v_ps1")
+        turn_values(2)
+        turn_values(3)
+        weave_values(0, "hi0", nc.vector.tensor_copy)
+        quantize_weights(0)
         weave_weights(1, "")
-        quantize_weights(1)
         quantize_values(0)
+        quantize_weights(1)
         gain = sb("gain", [P, Q], F32)
         nc.scalar.activation(gain[:], g_pool[:].indirect(list4[:]), COPY)
-        weave_values(1, "g_pool", nc.scalar.copy)
+        weave_values(1, "", nc.vector.tensor_copy)
         quantize_values(1)
-        product(0, "v_ps1")
+        product(0, "w_ps0")
         product(1, "acc0")
         for b in range(EB):
             pick_member(b)

@@ -19,6 +19,11 @@ COPY = mybir.ActivationFunctionType.Copy
 P = 128
 PACK = 4
 BANK = 512
+QUAD = 32
+ROWS = 4
+GROUP = 16
+LINE = 4
+PAIR = 2
 QT = Q // P
 EB = E // P
 CH = T // BANK
@@ -51,11 +56,11 @@ def tile_attend_middle_bymember_lean_kernel(
             nc.sync.dma_start(q_raw[j][:], query[:, P * j : P * (j + 1)].rearrange("(p t) q -> p t q", t=PACK))
 
         load_query(0)
-        for quad in range(4):
-            rows = keys_scales[0][4 * quad : 4 * quad + 4, :].bitcast(I32)
-            queue = nc.sync if quad < 2 else nc.scalar
+        for quad in range(P // QUAD):
+            rows = keys_scales[0][ROWS * quad : ROWS * (quad + 1), :].bitcast(I32)
+            queue = nc.sync if quad < P // QUAD // 2 else nc.scalar
             queue.dma_start(
-                k_scales[32 * quad : 32 * quad + 16, :].bitcast(I32),
+                k_scales[QUAD * quad : QUAD * quad + ROWS * CH, :].bitcast(I32),
                 rows.rearrange("r (c n) -> c r n", c=CH),
             )
         for c in range(CH):
@@ -65,7 +70,7 @@ def tile_attend_middle_bymember_lean_kernel(
         load_query(1)
         lists = []
         for n, src in enumerate((offs, offs2, offs3)):
-            lists.append(keep.tile([P, I // 16], U16, name=f"list{n}"))
+            lists.append(keep.tile([P, I // GROUP], U16, name=f"list{n}"))
             nc.sync.dma_start(lists[n][:], src)
         v_pool = [sb(f"v_pool{b}", [P, T], F32) for b in range(EB)]
         m_pool = [sb(f"m_pool{b}", [P, M], F32) for b in range(EB)]
@@ -79,7 +84,7 @@ def tile_attend_middle_bymember_lean_kernel(
         load_values(0)
         os_col = sb("os_col", [P, PACK], F32)
         nc.sync.dma_start(os_col[:], slot_factor.rearrange("o (p t) -> (o p) t", t=PACK))
-        list4 = keep.tile([P, Q // 16], U16, name="list4")
+        list4 = keep.tile([P, Q // GROUP], U16, name="list4")
         nc.sync.dma_start(list4[:], offs4)
         for b in range(1, EB):
             load_values(b)
@@ -95,10 +100,16 @@ def tile_attend_middle_bymember_lean_kernel(
         def quantize(codes, scales, src):
             nc.vector.quantize_mx(out=codes.bitcast(FP8X4), scales=scales, in_=src)
 
+        def copy_on(on_vector, dst, src):
+            if on_vector:
+                nc.vector.tensor_copy(dst, src)
+            else:
+                nc.scalar.activation(dst, src, COPY)
+
         def prepare_query(j):
             nc.vector.tensor_copy(
-                q_bf[j][:].rearrange("p (c n) t -> p c t n", n=4),
-                q_raw[j][:].rearrange("p t (c n) -> p c t n", n=4),
+                q_bf[j][:].rearrange("p (c n) t -> p c t n", n=LINE),
+                q_raw[j][:].rearrange("p t (c n) -> p c t n", n=LINE),
             )
             quantize(q_codes[j][:], q_scales[j][:], q_bf[j][:].rearrange("p q t -> p (q t)"))
 
@@ -113,23 +124,15 @@ def tile_attend_middle_bymember_lean_kernel(
                 lhsT=q_codes[j][:].bitcast(FP8X4),
                 lhsT_scale=q_scales[j][:],
                 rhs=k_words[c][:, cols].bitcast(FP8X4),
-                rhs_scale=k_scales[4 * c :, cols],
+                rhs_scale=k_scales[ROWS * c :, cols],
                 start=True,
                 stop=True,
             )
-            dst = a_sb[j][:, BANK * c + first : BANK * c + first + width]
-            if on_vector:
-                nc.vector.tensor_copy(dst, acc[:])
-            else:
-                nc.scalar.activation(dst, acc[:], COPY)
+            copy_on(on_vector, a_sb[j][:, BANK * c + first : BANK * c + first + width], acc[:])
 
         def pick(j, n, on_vector, tag=""):
             picked[j][n] = sb(f"picked{j}_{n}", [P, I], F32, tag)
-            src = a_sb[j][:].indirect(lists[n][:])
-            if on_vector:
-                nc.vector.tensor_copy(picked[j][n][:], src)
-            else:
-                nc.scalar.activation(picked[j][n][:], src, COPY)
+            copy_on(on_vector, picked[j][n][:], a_sb[j][:].indirect(lists[n][:]))
 
         w_bf = {}
         w_codes = sb("w_codes", [P, Q], U32)
@@ -187,42 +190,38 @@ def tile_attend_middle_bymember_lean_kernel(
             )
 
         v_in = {}
-        v_codes = [sb(f"v_codes{g}", [P, 2 * P], U32) for g in range(2)]
-        v_scales = [sb(f"v_scales{g}", [P, 2 * P], U8) for g in range(2)]
+        v_codes = [sb(f"v_codes{g}", [P, PAIR * P], U32) for g in range(EB // PAIR)]
+        v_scales = [sb(f"v_scales{g}", [P, PAIR * P], U8) for g in range(EB // PAIR)]
 
         v_ps = {}
         v_bf = {}
 
         def pick_values(b, on_vector, tag):
             v_bf[b] = sb(f"v_bf{b}", [P, I], BF16, tag)
-            src = v_pool[b][:].indirect(lists[0][:])
-            if on_vector:
-                nc.vector.tensor_copy(v_bf[b][:], src)
-            else:
-                nc.scalar.activation(v_bf[b][:], src, COPY)
+            copy_on(on_vector, v_bf[b][:], v_pool[b][:].indirect(lists[0][:]))
 
         def turn_values(b):
             words = v_bf[b][:].bitcast(F32)
             for u in range(2):
-                nc.tensor.transpose(v_ps[b // 2][:, b % 2, u, :], words[:, u::2], ident[:])
+                nc.tensor.transpose(v_ps[b // PAIR][:, b % PAIR, u, :], words[:, u::2], ident[:])
 
         def weave_values(g, tag, copy):
-            v_in[g] = sb(f"v_in{g}", [P, 2, P, 2], F32, tag)
+            v_in[g] = sb(f"v_in{g}", [P, PAIR, P, 2], F32, tag)
             copy(v_in[g][:], v_ps[g][:].rearrange("p x u e -> p x e u"))
 
         def quantize_values(g):
             quantize(v_codes[g][:], v_scales[g][:], v_in[g][:].rearrange("p x e u -> p (x e u)").bitcast(BF16))
 
-        m_picked = [sb(f"m_picked{g}", [P, 2, Q], F32) for g in range(2)]
-        scaled = [sb(f"scaled{g}", [P, 2, Q], F32) for g in range(2)]
-        result = [sb(f"result{g}", [P, 2, Q], F32) for g in range(2)]
+        m_picked = [sb(f"m_picked{g}", [P, PAIR, Q], F32) for g in range(EB // PAIR)]
+        scaled = [sb(f"scaled{g}", [P, PAIR, Q], F32) for g in range(EB // PAIR)]
+        result = [sb(f"result{g}", [P, PAIR, Q], F32) for g in range(EB // PAIR)]
 
         def pick_member(b):
-            nc.scalar.activation(m_picked[b // 2][:, b % 2, :], m_pool[b][:].indirect(list4[:]), COPY)
+            nc.scalar.activation(m_picked[b // PAIR][:, b % PAIR, :], m_pool[b][:].indirect(list4[:]), COPY)
 
         def product(g, tag):
-            acc = bank(tag, [P, 2, Q], f"o_ps{g}")
-            for x in range(2):
+            acc = bank(tag, [P, PAIR, Q], f"o_ps{g}")
+            for x in range(PAIR):
                 nc.tensor.matmul_mx(
                     out=acc[:, x, :],
                     lhsT=v_codes[g][:, P * x : P * (x + 1)].bitcast(FP8X4),
@@ -233,17 +232,17 @@ def tile_attend_middle_bymember_lean_kernel(
                     stop=True,
                 )
             nc.vector.tensor_tensor(
-                scaled[g][:], acc[:], gain[:].unsqueeze(1).to_broadcast([P, 2, Q]), ALU.mult
+                scaled[g][:], acc[:], gain[:].unsqueeze(1).to_broadcast([P, PAIR, Q]), ALU.mult
             )
 
         def finish(b):
-            g, x = divmod(b, 2)
+            g, x = divmod(b, PAIR)
             nc.vector.tensor_tensor(result[g][:, x, :], scaled[g][:, x, :], m_picked[g][:, x, :], ALU.add)
             nc.sync.dma_start(out[P * b : P * (b + 1), :], result[g][:, x, :])
 
         prepare_query(0)
         for c in range(CH - 1):
-            scores(0, c, c != 1)
+            scores(0, c, c % 2 == 0)
         scores(0, CH - 1, False, 0, BANK // 2)
         scores(0, CH - 1, False, BANK // 2, BANK // 2, "acc4")
         prepare_query(1)
@@ -252,12 +251,12 @@ def tile_attend_middle_bymember_lean_kernel(
         scale_second(0)
         pick(0, 2, False)
         for c in range(CH):
-            scores(1, c, c < 2)
+            scores(1, c, c < CH // 2)
         larger(0, "")
         smaller(0, "")
         cap(0)
         median(0)
-        v_ps[0] = bank("acc4", [P, 2, 2, P], "v_ps0")
+        v_ps[0] = bank("acc4", [P, PAIR, 2, P], "v_ps0")
         pick_values(0, True, "picked0_2")
         turn_values(0)
         pick(1, 1, False)
@@ -273,7 +272,7 @@ def tile_attend_middle_bymember_lean_kernel(
         pick_values(2, False, "picked0_2")
         pick_values(3, False, "v_pool1")
         weave_weights(0, "picked1_2")
-        v_ps[1] = bank("w_ps0", [P, 2, 2, P], "v_ps1")
+        v_ps[1] = bank("w_ps0", [P, PAIR, 2, P], "v_ps1")
         turn_values(2)
         turn_values(3)
         weave_values(0, "hi0", nc.vector.tensor_copy)
@@ -283,7 +282,7 @@ def tile_attend_middle_bymember_lean_kernel(
         quantize_weights(1)
         gain = sb("gain", [P, Q], F32)
         nc.scalar.activation(gain[:], g_pool[:].indirect(list4[:]), COPY)
-        weave_values(1, "", nc.vector.tensor_copy)
+        weave_values(1, "g_pool", nc.scalar.copy)
         quantize_values(1)
         product(0, "w_ps0")
         product(1, "acc0")

from contextlib import ExitStack

import concourse.mybir as mybir
from concourse.masks import make_identity

D, T, I, Q, E, M = 512, 2048, 512, 256, 512, 1024
FLOPS = 2 * D * Q * T + 2 * I * E * Q

F32 = mybir.dt.float32
BF16 = mybir.dt.bfloat16
U32 = mybir.dt.uint32
I32 = mybir.dt.int32
U16 = mybir.dt.uint16
U8 = mybir.dt.uint8
FP8X4 = mybir.dt.float8_e4m3fn_x4
ALU = mybir.AluOpType
COPY = mybir.ActivationFunctionType.Copy

P = 128
PACK = 4
BANK = 512
QUAD = 32
ROWS = 4
GROUP = 16
LINE = 4
PAIR = 2
QT = Q // P
EB = E // P
CH = T // BANK


def tile_attend_middle_bymember_lean_kernel(
    tc, query, keys_words, keys_scales, lam, slot_factor, vals, member, mgain, offs, offs2, offs3, offs4, out
):
    nc = tc.nc
    with ExitStack() as ctx:
        keep = ctx.enter_context(tc.tile_pool(name="keep", bufs=1))
        psum = ctx.enter_context(tc.psum_pool(name="psum", bufs=1))

        def sb(name, shape, dtype, tag=""):
            return keep.tile(shape, dtype, name=name, tag=tag or name, align_bytes=64)

        def bank(tag, shape, name):
            return psum.tile(shape, F32, name=name, tag=tag)

        k_scales = sb("k_scales", [P, BANK], U8)
        nc.gpsimd.memset(k_scales[:].bitcast(I32), 0)
        ident = sb("ident", [P, P], F32)
        make_identity(nc, ident[:])

        q_raw = [sb(f"q_raw{j}", [P, PACK, P], F32) for j in range(QT)]
        k_words = [sb(f"k_words{c}", [P, BANK], U32) for c in range(CH)]
        k_flat = keys_words[0].rearrange("p n t -> p (n t)")

        def load_query(j):
            nc.sync.dma_start(q_raw[j][:], query[:, P * j : P * (j + 1)].rearrange("(p t) q -> p t q", t=PACK))

        load_query(0)
        for quad in range(P // QUAD):
            rows = keys_scales[0][ROWS * quad : ROWS * (quad + 1), :].bitcast(I32)
            queue = nc.sync if quad < P // QUAD // 2 else nc.scalar
            queue.dma_start(
                k_scales[QUAD * quad : QUAD * quad + ROWS * CH, :].bitcast(I32),
                rows.rearrange("r (c n) -> c r n", c=CH),
            )
        for c in range(CH):
            nc.sync.dma_start(
                k_words[c][:].bitcast(I32), k_flat[:, PACK * BANK * c : PACK * BANK * (c + 1)].bitcast(I32)
            )
        load_query(1)
        lists = []
        for n, src in enumerate((offs, offs2, offs3)):
            lists.append(keep.tile([P, I // GROUP], U16, name=f"list{n}"))
            nc.sync.dma_start(lists[n][:], src)
        v_pool = [sb(f"v_pool{b}", [P, T], F32) for b in range(EB)]
        m_pool = [sb(f"m_pool{b}", [P, M], F32) for b in range(EB)]

        def load_values(b):
            nc.sync.dma_start(v_pool[b][:], vals[P * b : P * (b + 1), :])

        lam_col = sb("lam_col", [P, QT], F32)
        with nc.allow_non_contiguous_dma(reason="one factor a partition"):
            nc.sync.dma_start(lam_col[:], lam.rearrange("(j p) o -> p (j o)", j=QT))
        load_values(0)
        os_col = sb("os_col", [P, PACK], F32)
        nc.sync.dma_start(os_col[:], slot_factor.rearrange("o (p t) -> (o p) t", t=PACK))
        list4 = keep.tile([P, Q // GROUP], U16, name="list4")
        nc.sync.dma_start(list4[:], offs4)
        for b in range(1, EB):
            load_values(b)
        g_pool = sb("g_pool", [P, M], F32)
        nc.sync.dma_start(g_pool[:], mgain)
        for b in range(EB):
            nc.sync.dma_start(m_pool[b][:], member[P * b : P * (b + 1), :])

        q_bf = [sb(f"q_bf{j}", [P, P, PACK], BF16) for j in range(QT)]
        q_codes = [sb(f"q_codes{j}", [P, P], U32) for j in range(QT)]
        q_scales = [sb(f"q_scales{j}", [P, P], U8) for j in range(QT)]

        def quantize(codes, scales, src):
            nc.vector.quantize_mx(out=codes.bitcast(FP8X4), scales=scales, in_=src)

        def copy_on(on_vector, dst, src):
            if on_vector:
                nc.vector.tensor_copy(dst, src)
            else:
                nc.scalar.activation(dst, src, COPY)

        def prepare_query(j):
            nc.vector.tensor_copy(
                q_bf[j][:].rearrange("p (c n) t -> p c t n", n=LINE),
                q_raw[j][:].rearrange("p t (c n) -> p c t n", n=LINE),
            )
            quantize(q_codes[j][:], q_scales[j][:], q_bf[j][:].rearrange("p q t -> p (q t)"))

        a_sb = [sb(f"a_sb{j}", [P, T], F32) for j in range(QT)]
        picked = [{} for j in range(QT)]

        def scores(j, c, on_vector, first=0, width=BANK, tag=""):
            acc = bank(tag or f"acc{c}", [P, width], f"a_ps{j}_{c}_{first}")
            cols = slice(first, first + width)
            nc.tensor.matmul_mx(
                out=acc[:],
                lhsT=q_codes[j][:].bitcast(FP8X4),
                lhsT_scale=q_scales[j][:],
                rhs=k_words[c][:, cols].bitcast(FP8X4),
                rhs_scale=k_scales[ROWS * c :, cols],
                start=True,
                stop=True,
            )
            copy_on(on_vector, a_sb[j][:, BANK * c + first : BANK * c + first + width], acc[:])

        def pick(j, n, on_vector, tag=""):
            picked[j][n] = sb(f"picked{j}_{n}", [P, I], F32, tag)
            copy_on(on_vector, picked[j][n][:], a_sb[j][:].indirect(lists[n][:]))

        w_bf = {}
        w_codes = sb("w_codes", [P, Q], U32)
        w_scales = sb("w_scales", [P, Q], U8)
        lo = {}
        hi = {}

        second = [sb(f"second{j}", [P, I], F32) for j in range(QT)]

        def scale_second(j):
            nc.gpsimd.tensor_scalar(second[j][:], picked[j][1][:], lam_col[:, j : j + 1], 0.0, ALU.mult, ALU.add)

        def scaled_against(dst, j, n, other, op):
            nc.vector.scalar_tensor_tensor(dst, picked[j][n][:], lam_col[:, j : j + 1], other, ALU.mult, op)

        def larger(j, tag):
            hi[j] = sb(f"hi{j}", [P, I], F32, tag)
            scaled_against(hi[j][:], j, 0, second[j][:], ALU.max)

        def smaller(j, tag):
            lo[j] = sb(f"lo{j}", [P, I], F32, tag)
            scaled_against(lo[j][:], j, 0, second[j][:], ALU.min)

        def cap(j):
            scaled_against(hi[j][:], j, 2, hi[j][:], ALU.min)

        middle = {}

        def median(j):
            middle[j] = sb(f"middle{j}", [P, 2, I // 2], F32)
            nc.vector.tensor_tensor(
                middle[j][:],
                lo[j][:].rearrange("p (m u) -> p u m", u=2),
                hi[j][:].rearrange("p (m u) -> p u m", u=2),
                ALU.max,
            )
            for t in range(PACK):
                nc.tensor.transpose(w_ps[j][:, t, :], middle[j][:, t % 2, t // 2 :: 2], ident[:])

        w_ps = [bank(f"w_ps{j}", [P, PACK, P], f"w_ps{j}") for j in range(QT)]

        def quantize_weights(j):
            cols = slice(P * j, P * (j + 1))
            quantize(w_codes[:, cols], w_scales[:, cols], w_bf[j][:].rearrange("p q t -> p (q t)"))

        def weave_weights(j, tag):
            w_bf[j] = sb(f"w_bf{j}", [P, P, PACK], BF16, tag)
            nc.vector.scalar_tensor_tensor(
                w_bf[j][:],
                w_ps[j][:].rearrange("p t q -> p q t"),
                0.0,
                os_col[:].unsqueeze(1).to_broadcast([P, P, PACK]),
                ALU.max,
                ALU.mult,
            )

        v_in = {}
        v_codes = [sb(f"v_codes{g}", [P, PAIR * P], U32) for g in range(EB // PAIR)]
        v_scales = [sb(f"v_scales{g}", [P, PAIR * P], U8) for g in range(EB // PAIR)]

        v_ps = {}
        v_bf = {}

        def pick_values(b, on_vector, tag):
            v_bf[b] = sb(f"v_bf{b}", [P, I], BF16, tag)
            copy_on(on_vector, v_bf[b][:], v_pool[b][:].indirect(lists[0][:]))

        def turn_values(b):
            words = v_bf[b][:].bitcast(F32)
            for u in range(2):
                nc.tensor.transpose(v_ps[b // PAIR][:, b % PAIR, u, :], words[:, u::2], ident[:])

        def weave_values(g, tag, copy):
            v_in[g] = sb(f"v_in{g}", [P, PAIR, P, 2], F32, tag)
            copy(v_in[g][:], v_ps[g][:].rearrange("p x u e -> p x e u"))

        def quantize_values(g):
            quantize(v_codes[g][:], v_scales[g][:], v_in[g][:].rearrange("p x e u -> p (x e u)").bitcast(BF16))

        m_picked = [sb(f"m_picked{g}", [P, PAIR, Q], F32) for g in range(EB // PAIR)]
        scaled = [sb(f"scaled{g}", [P, PAIR, Q], F32) for g in range(EB // PAIR)]
        result = [sb(f"result{g}", [P, PAIR, Q], F32) for g in range(EB // PAIR)]

        def pick_member(b):
            nc.scalar.activation(m_picked[b // PAIR][:, b % PAIR, :], m_pool[b][:].indirect(list4[:]), COPY)

        def product(g, tag):
            acc = bank(tag, [P, PAIR, Q], f"o_ps{g}")
            for x in range(PAIR):
                nc.tensor.matmul_mx(
                    out=acc[:, x, :],
                    lhsT=v_codes[g][:, P * x : P * (x + 1)].bitcast(FP8X4),
                    lhsT_scale=v_scales[g][:, P * x : P * (x + 1)],
                    rhs=w_codes[:].bitcast(FP8X4),
                    rhs_scale=w_scales[:],
                    start=True,
                    stop=True,
                )
            nc.vector.tensor_tensor(
                scaled[g][:], acc[:], gain[:].unsqueeze(1).to_broadcast([P, PAIR, Q]), ALU.mult
            )

        def finish(b):
            g, x = divmod(b, PAIR)
            nc.vector.tensor_tensor(result[g][:, x, :], scaled[g][:, x, :], m_picked[g][:, x, :], ALU.add)
            nc.sync.dma_start(out[P * b : P * (b + 1), :], result[g][:, x, :])

        prepare_query(0)
        for c in range(CH - 1):
            scores(0, c, c % 2 == 0)
        scores(0, CH - 1, False, 0, BANK // 2)
        scores(0, CH - 1, False, BANK // 2, BANK // 2, "acc4")
        prepare_query(1)
        pick(0, 0, True, "q_bf1")
        pick(0, 1, False)
        scale_second(0)
        pick(0, 2, False)
        for c in range(CH):
            scores(1, c, c < CH // 2)
        larger(0, "")
        smaller(0, "")
        cap(0)
        median(0)
        v_ps[0] = bank("acc4", [P, PAIR, 2, P], "v_ps0")
        pick_values(0, True, "picked0_2")
        turn_values(0)
        pick(1, 1, False)
        scale_second(1)
        pick(1, 0, False)
        pick(1, 2, False)
        larger(1, "lo0")
        smaller(1, "hi0")
        cap(1)
        median(1)
        pick_values(1, False, "v_pool0")
        turn_values(1)
        pick_values(2, False, "picked0_2")
        pick_values(3, False, "v_pool1")
        weave_weights(0, "picked1_2")
        v_ps[1] = bank("w_ps0", [P, PAIR, 2, P], "v_ps1")
        turn_values(2)
        turn_values(3)
        weave_values(0, "hi0", nc.vector.tensor_copy)
        quantize_weights(0)
        weave_weights(1, "")
        quantize_values(0)
        quantize_weights(1)
        gain = sb("gain", [P, Q], F32)
        nc.scalar.activation(gain[:], g_pool[:].indirect(list4[:]), COPY)
        weave_values(1, "g_pool", nc.scalar.copy)
        quantize_values(1)
        product(0, "w_ps0")
        product(1, "acc0")
        for b in range(EB):
            pick_member(b)
        for b in range(EB):
            finish(b)
